import numpy as np
CORES = [4,12,20,28,36,44,52,60,68,76,84,92,100,108,116,124]
N = 16
def setup_inputs(rng):
    return {"x": rng.standard_normal((N, 128, 1), dtype=np.float32)}
def reference(x):
    s = x.sum(axis=0, dtype=np.float64).astype(x.dtype)
    return {"y": np.broadcast_to(s, (N,) + s.shape)}

@@ -1,0 +1,48 @@
+from concourse.bass import DstId, RemoteDMATransfer
+
+SCRATCH = {
+    "xs": ("sbuf", [128, 1], "float32"),
+    "land": ("sbuf", [128, 8], "float32"),
+    "sq": ("sbuf", [128, 1], "float32"),
+    "tot": ("sbuf", [128, 1], "float32"),
+}
+SEMAPHORES = ["loaded", "sent", "arr1", "arr2", "arr3", "stored"]
+
+RANK_CORE = 4
+HELPER = 6
+
+
+def rank_program(g, core, T, topo):
+    chip, k = divmod(core, 8)
+
+    def dst(c):
+        rid, pid, _se = topo.addr(c)
+        return DstId(rid=rid, pnc=pid)
+
+    if k == RANK_CORE:
+        g.dma_start(T.xs[:], T.x[:]).then_inc(T.sem.loaded, 16)
+        g.wait_ge(T.sem.loaded, 16)
+        slot = chip // 2
+        peers = [ch for ch in range(16) if (ch & 1) == (chip & 1)]
+        g.remote_dma_fused(
+            [RemoteDMATransfer(dst_ids=[dst(ch * 8 + HELPER)], dma_engine_mask=1 << i, remote_sem=T.sem.arr1,
+                               src=T.xs[:], dst=T.land[:, slot:slot + 1])
+             for i, ch in enumerate(peers)],
+            local_sem=T.sem.sent)
+        g.wait_ge(T.sem.arr3, 1)
+        g.dma_start(T.y[:], T.tot[:]).then_inc(T.sem.stored, 16)
+        g.wait_ge(T.sem.stored, 16)
+        g.wait_ge(T.sem.sent, 8)
+    elif k == HELPER:
+        cols = [T.land[:, j:j + 1] for j in range(8)]
+        g.wait_ge(T.sem.arr1, 8)
+        g.remote_dma_fused(
+            [RemoteDMATransfer(dst_ids=[dst((chip ^ 1) * 8 + HELPER)], dma_engine_mask=1, remote_sem=T.sem.arr2,
+                               srcs=cols, dsts=[T.sq[:]], alu_op=1)],
+            local_sem=T.sem.sent)
+        g.wait_ge(T.sem.arr2, 1)
+        g.remote_dma_fused(
+            [RemoteDMATransfer(dst_ids=[dst(chip * 8 + RANK_CORE)], dma_engine_mask=1, remote_sem=T.sem.arr3,
+                               srcs=cols + [T.sq[:]], dsts=[T.tot[:]], alu_op=1)],
+            local_sem=T.sem.sent)
+        g.wait_ge(T.sem.sent, 2)

@@ -1,10 +1,10 @@
 from concourse.bass import DstId, RemoteDMATransfer
 
 SCRATCH = {
-    "xs": ("sbuf", [128, 1], "float32"),
-    "land": ("sbuf", [128, 8], "float32"),
-    "sq": ("sbuf", [128, 1], "float32"),
-    "tot": ("sbuf", [128, 1], "float32"),
+    "xs": ("dram", [128, 1], "float32"),
+    "land": ("dram", [8, 128, 1], "float32"),
+    "sq": ("dram", [128, 1], "float32"),
+    "tot": ("dram", [128, 1], "float32"),
 }
 SEMAPHORES = ["loaded", "sent", "arr1", "arr2", "arr3", "stored"]
 
@@ -26,7 +26,7 @@ def rank_program(g, core, T, topo):
         peers = [ch for ch in range(16) if (ch & 1) == (chip & 1)]
         g.remote_dma_fused(
             [RemoteDMATransfer(dst_ids=[dst(ch * 8 + HELPER)], dma_engine_mask=1 << i, remote_sem=T.sem.arr1,
-                               src=T.xs[:], dst=T.land[:, slot:slot + 1])
+                               src=T.xs[:], dst=T.land[slot])
              for i, ch in enumerate(peers)],
             local_sem=T.sem.sent)
         g.wait_ge(T.sem.arr3, 1)
@@ -34,15 +34,15 @@ def rank_program(g, core, T, topo):
         g.wait_ge(T.sem.stored, 16)
         g.wait_ge(T.sem.sent, 8)
     elif k == HELPER:
-        cols = [T.land[:, j:j + 1] for j in range(8)]
+        slots = [T.land[j] for j in range(8)]
         g.wait_ge(T.sem.arr1, 8)
         g.remote_dma_fused(
             [RemoteDMATransfer(dst_ids=[dst((chip ^ 1) * 8 + HELPER)], dma_engine_mask=1, remote_sem=T.sem.arr2,
-                               srcs=cols, dsts=[T.sq[:]], alu_op=1)],
+                               srcs=slots, dsts=[T.sq[:]], alu_op=1)],
             local_sem=T.sem.sent)
         g.wait_ge(T.sem.arr2, 1)
         g.remote_dma_fused(
             [RemoteDMATransfer(dst_ids=[dst(chip * 8 + RANK_CORE)], dma_engine_mask=1, remote_sem=T.sem.arr3,
-                               srcs=cols + [T.sq[:]], dsts=[T.tot[:]], alu_op=1)],
+                               srcs=slots + [T.sq[:]], dsts=[T.tot[:]], alu_op=1)],
             local_sem=T.sem.sent)
         g.wait_ge(T.sem.sent, 2)

@@ -1,12 +1,13 @@
 from concourse.bass import DstId, RemoteDMATransfer
+from concourse.mybir import AluOpType
 
 SCRATCH = {
     "xs": ("dram", [128, 1], "float32"),
     "land": ("dram", [8, 128, 1], "float32"),
+    "sp": ("dram", [128, 1], "float32"),
     "sq": ("dram", [128, 1], "float32"),
-    "tot": ("dram", [128, 1], "float32"),
 }
-SEMAPHORES = ["loaded", "sent", "arr1", "arr2", "arr3", "stored"]
+SEMAPHORES = ["loaded", "sent", "arr1", "own", "mate", "stored"]
 
 RANK_CORE = 4
 HELPER = 6
@@ -29,20 +30,20 @@ def rank_program(g, core, T, topo):
                                src=T.xs[:], dst=T.land[slot])
              for i, ch in enumerate(peers)],
             local_sem=T.sem.sent)
-        g.wait_ge(T.sem.arr3, 1)
-        g.dma_start(T.y[:], T.tot[:]).then_inc(T.sem.stored, 16)
+        g.wait_ge(T.sem.own, 1)
+        g.dma_start(T.y[:], T.sp[:]).then_inc(T.sem.stored, 16)
+        g.wait_ge(T.sem.mate, 1)
         g.wait_ge(T.sem.stored, 16)
+        g.dma_start(T.y[:], T.sq[:], accum_op=AluOpType.add).then_inc(T.sem.stored, 16)
+        g.wait_ge(T.sem.stored, 32)
         g.wait_ge(T.sem.sent, 8)
     elif k == HELPER:
         slots = [T.land[j] for j in range(8)]
         g.wait_ge(T.sem.arr1, 8)
         g.remote_dma_fused(
-            [RemoteDMATransfer(dst_ids=[dst((chip ^ 1) * 8 + HELPER)], dma_engine_mask=1, remote_sem=T.sem.arr2,
-                               srcs=slots, dsts=[T.sq[:]], alu_op=1)],
-            local_sem=T.sem.sent)
-        g.wait_ge(T.sem.arr2, 1)
-        g.remote_dma_fused(
-            [RemoteDMATransfer(dst_ids=[dst(chip * 8 + RANK_CORE)], dma_engine_mask=1, remote_sem=T.sem.arr3,
-                               srcs=slots + [T.sq[:]], dsts=[T.tot[:]], alu_op=1)],
+            [RemoteDMATransfer(dst_ids=[dst((chip ^ 1) * 8 + RANK_CORE)], dma_engine_mask=1, remote_sem=T.sem.mate,
+                               srcs=slots, dsts=[T.sq[:]], alu_op=1),
+             RemoteDMATransfer(dst_ids=[dst(chip * 8 + RANK_CORE)], dma_engine_mask=2, remote_sem=T.sem.own,
+                               srcs=slots, dsts=[T.sp[:]], alu_op=1)],
             local_sem=T.sem.sent)
         g.wait_ge(T.sem.sent, 2)

@@ -26,24 +26,23 @@ def rank_program(g, core, T, topo):
         slot = chip // 2
         peers = [ch for ch in range(16) if (ch & 1) == (chip & 1)]
         g.remote_dma_fused(
-            [RemoteDMATransfer(dst_ids=[dst(ch * 8 + HELPER)], dma_engine_mask=1 << i, remote_sem=T.sem.arr1,
-                               src=T.xs[:], dst=T.land[slot])
-             for i, ch in enumerate(peers)],
+            [RemoteDMATransfer(dst_ids=[dst(ch * 8 + HELPER) for ch in peers], dma_engine_mask=0xFF,
+                               remote_sem=T.sem.arr1, srcs=[T.xs[:]], dsts=[T.land[slot] for _ch in peers])],
             local_sem=T.sem.sent)
+        g.wait_ge(T.sem.sent, 8)
         g.wait_ge(T.sem.own, 1)
         g.dma_start(T.y[:], T.sp[:]).then_inc(T.sem.stored, 16)
         g.wait_ge(T.sem.mate, 1)
         g.wait_ge(T.sem.stored, 16)
         g.dma_start(T.y[:], T.sq[:], accum_op=AluOpType.add).then_inc(T.sem.stored, 16)
         g.wait_ge(T.sem.stored, 32)
-        g.wait_ge(T.sem.sent, 8)
     elif k == HELPER:
         slots = [T.land[j] for j in range(8)]
-        g.wait_ge(T.sem.arr1, 8)
+        g.wait_ge(T.sem.arr1, 64)
         g.remote_dma_fused(
-            [RemoteDMATransfer(dst_ids=[dst((chip ^ 1) * 8 + RANK_CORE)], dma_engine_mask=1, remote_sem=T.sem.mate,
-                               srcs=slots, dsts=[T.sq[:]], alu_op=1),
-             RemoteDMATransfer(dst_ids=[dst(chip * 8 + RANK_CORE)], dma_engine_mask=2, remote_sem=T.sem.own,
-                               srcs=slots, dsts=[T.sp[:]], alu_op=1)],
+            [RemoteDMATransfer(dst_ids=[dst(chip * 8 + RANK_CORE)], dma_engine_mask=1, remote_sem=T.sem.own,
+                               srcs=slots, dsts=[T.sp[:]], alu_op=1),
+             RemoteDMATransfer(dst_ids=[dst((chip ^ 1) * 8 + RANK_CORE)], dma_engine_mask=2, remote_sem=T.sem.mate,
+                               srcs=slots, dsts=[T.sq[:]], alu_op=1)],
             local_sem=T.sem.sent)
         g.wait_ge(T.sem.sent, 2)

@@ -24,15 +24,15 @@ def rank_program(g, core, T, topo):
         g.dma_start(T.xs[:], T.x[:]).then_inc(T.sem.loaded, 16)
         g.wait_ge(T.sem.loaded, 16)
         slot = chip // 2
-        peers = [ch for ch in range(16) if (ch & 1) == (chip & 1)]
+        peers = [(chip + 2 * j) % 16 for j in range(1, 9)]
         g.remote_dma_fused(
             [RemoteDMATransfer(dst_ids=[dst(ch * 8 + HELPER) for ch in peers], dma_engine_mask=0xFF,
                                remote_sem=T.sem.arr1, srcs=[T.xs[:]], dsts=[T.land[slot] for _ch in peers])],
             local_sem=T.sem.sent)
         g.wait_ge(T.sem.sent, 8)
-        g.wait_ge(T.sem.own, 1)
+        g.wait_ge(T.sem.own, 8)
         g.dma_start(T.y[:], T.sp[:]).then_inc(T.sem.stored, 16)
-        g.wait_ge(T.sem.mate, 1)
+        g.wait_ge(T.sem.mate, 8)
         g.wait_ge(T.sem.stored, 16)
         g.dma_start(T.y[:], T.sq[:], accum_op=AluOpType.add).then_inc(T.sem.stored, 16)
         g.wait_ge(T.sem.stored, 32)
@@ -40,9 +40,9 @@ def rank_program(g, core, T, topo):
         slots = [T.land[j] for j in range(8)]
         g.wait_ge(T.sem.arr1, 64)
         g.remote_dma_fused(
-            [RemoteDMATransfer(dst_ids=[dst(chip * 8 + RANK_CORE)], dma_engine_mask=1, remote_sem=T.sem.own,
+            [RemoteDMATransfer(dst_ids=[dst(chip * 8 + RANK_CORE)], dma_engine_mask=0xFF00, remote_sem=T.sem.own,
                                srcs=slots, dsts=[T.sp[:]], alu_op=1),
-             RemoteDMATransfer(dst_ids=[dst((chip ^ 1) * 8 + RANK_CORE)], dma_engine_mask=2, remote_sem=T.sem.mate,
-                               srcs=slots, dsts=[T.sq[:]], alu_op=1)],
+             RemoteDMATransfer(dst_ids=[dst((chip ^ 1) * 8 + RANK_CORE)], dma_engine_mask=0x00FF,
+                               remote_sem=T.sem.mate, srcs=slots, dsts=[T.sq[:]], alu_op=1)],
             local_sem=T.sem.sent)
-        g.wait_ge(T.sem.sent, 2)
+        g.wait_ge(T.sem.sent, 16)

@@ -1,13 +1,12 @@
 from concourse.bass import DstId, RemoteDMATransfer
-from concourse.mybir import AluOpType
 
 SCRATCH = {
     "xs": ("dram", [128, 1], "float32"),
     "land": ("dram", [8, 128, 1], "float32"),
-    "sp": ("dram", [128, 1], "float32"),
     "sq": ("dram", [128, 1], "float32"),
+    "tot": ("dram", [128, 1], "float32"),
 }
-SEMAPHORES = ["loaded", "sent", "arr1", "own", "mate", "stored"]
+SEMAPHORES = ["loaded", "sent", "arr1", "arr2", "arr3", "stored"]
 
 RANK_CORE = 4
 HELPER = 6
@@ -30,19 +29,19 @@ def rank_program(g, core, T, topo):
                                remote_sem=T.sem.arr1, srcs=[T.xs[:]], dsts=[T.land[slot] for _ch in peers])],
             local_sem=T.sem.sent)
         g.wait_ge(T.sem.sent, 8)
-        g.wait_ge(T.sem.own, 8)
-        g.dma_start(T.y[:], T.sp[:]).then_inc(T.sem.stored, 16)
-        g.wait_ge(T.sem.mate, 8)
+        g.wait_ge(T.sem.arr3, 16)
+        g.dma_start(T.y[:], T.tot[:]).then_inc(T.sem.stored, 16)
         g.wait_ge(T.sem.stored, 16)
-        g.dma_start(T.y[:], T.sq[:], accum_op=AluOpType.add).then_inc(T.sem.stored, 16)
-        g.wait_ge(T.sem.stored, 32)
     elif k == HELPER:
         slots = [T.land[j] for j in range(8)]
         g.wait_ge(T.sem.arr1, 64)
         g.remote_dma_fused(
-            [RemoteDMATransfer(dst_ids=[dst(chip * 8 + RANK_CORE)], dma_engine_mask=0xFF00, remote_sem=T.sem.own,
-                               srcs=slots, dsts=[T.sp[:]], alu_op=1),
-             RemoteDMATransfer(dst_ids=[dst((chip ^ 1) * 8 + RANK_CORE)], dma_engine_mask=0x00FF,
-                               remote_sem=T.sem.mate, srcs=slots, dsts=[T.sq[:]], alu_op=1)],
+            [RemoteDMATransfer(dst_ids=[dst((chip ^ 1) * 8 + HELPER)], dma_engine_mask=0x00FF, remote_sem=T.sem.arr2,
+                               srcs=slots, dsts=[T.sq[:]], alu_op=1)],
             local_sem=T.sem.sent)
-        g.wait_ge(T.sem.sent, 16)
+        g.wait_ge(T.sem.arr2, 8)
+        g.remote_dma_fused(
+            [RemoteDMATransfer(dst_ids=[dst(chip * 8 + RANK_CORE)], dma_engine_mask=0xFFFF, remote_sem=T.sem.arr3,
+                               srcs=slots + [T.sq[:]], dsts=[T.tot[:]], alu_op=1)],
+            local_sem=T.sem.sent)
+        g.wait_ge(T.sem.sent, 24)

from concourse.bass import DstId, RemoteDMATransfer

SCRATCH = {
    "xs": ("dram", [128, 1], "float32"),
    "land": ("dram", [8, 128, 1], "float32"),
    "sq": ("dram", [128, 1], "float32"),
    "tot": ("dram", [128, 1], "float32"),
}
SEMAPHORES = ["loaded", "sent", "arr1", "arr2", "arr3", "stored"]

RANK_CORE = 4
HELPER = 6


def rank_program(g, core, T, topo):
    chip, k = divmod(core, 8)

    def dst(c):
        rid, pid, _se = topo.addr(c)
        return DstId(rid=rid, pnc=pid)

    if k == RANK_CORE:
        g.dma_start(T.xs[:], T.x[:]).then_inc(T.sem.loaded, 16)
        g.wait_ge(T.sem.loaded, 16)
        slot = chip // 2
        peers = [(chip + 2 * j) % 16 for j in range(1, 9)]
        g.remote_dma_fused(
            [RemoteDMATransfer(dst_ids=[dst(ch * 8 + HELPER) for ch in peers], dma_engine_mask=0xFF,
                               remote_sem=T.sem.arr1, srcs=[T.xs[:]], dsts=[T.land[slot] for _ch in peers])],
            local_sem=T.sem.sent)
        g.wait_ge(T.sem.sent, 8)
        g.wait_ge(T.sem.arr3, 16)
        g.dma_start(T.y[:], T.tot[:]).then_inc(T.sem.stored, 16)
        g.wait_ge(T.sem.stored, 16)
    elif k == HELPER:
        slots = [T.land[j] for j in range(8)]
        g.wait_ge(T.sem.arr1, 64)
        g.remote_dma_fused(
            [RemoteDMATransfer(dst_ids=[dst((chip ^ 1) * 8 + HELPER)], dma_engine_mask=0x00FF, remote_sem=T.sem.arr2,
                               srcs=slots, dsts=[T.sq[:]], alu_op=1)],
            local_sem=T.sem.sent)
        g.wait_ge(T.sem.arr2, 8)
        g.remote_dma_fused(
            [RemoteDMATransfer(dst_ids=[dst(chip * 8 + RANK_CORE)], dma_engine_mask=0xFFFF, remote_sem=T.sem.arr3,
                               srcs=slots + [T.sq[:]], dsts=[T.tot[:]], alu_op=1)],
            local_sem=T.sem.sent)
        g.wait_ge(T.sem.sent, 24)
